import numpy as np
import ml_dtypes


def mxq(x, axis, fmt="e4m3"):
    dtype, down = {"e4m3": (ml_dtypes.float8_e4m3fn, 7), "e5m2": (ml_dtypes.float8_e5m2, 14)}[fmt]
    v = np.moveaxis(np.asarray(x, np.float32).astype(ml_dtypes.bfloat16).astype(np.float64), axis, -1)
    blocks = v.reshape(v.shape[:-1] + (-1, 32))
    amax = np.abs(blocks).max(-1, keepdims=True)
    byte = np.maximum(np.where(amax > 0, np.frexp(amax)[1] - 1 + 127, 0) - down, 1)
    scale = np.exp2(byte - 127.0)
    codes = (blocks / scale).astype(np.float32).astype(dtype).astype(np.float64)
    return np.moveaxis((codes * scale).reshape(v.shape), -1, axis)


WIDE = False


def mx_kscale(k):
    if not WIDE:
        return np.ones(k)
    levels = np.array([10, -10, 5, -5, 0])
    if k % 512:
        return np.exp2(np.random.permutation(np.resize(levels, k // 32))).repeat(32)
    a = np.empty((k // 512, 16))
    for p in range(k // 512):
        a[p, :8] = np.random.permutation(np.resize(levels, 8))
        for g in range(8):
            far = levels[np.abs(levels - a[p, g]) >= 10]
            a[p, g + 8] = far[np.random.randint(len(far))]
    return np.exp2(a.ravel()).repeat(32)


def f64(x):
    return np.asarray(x).astype(np.float64)


def striped(idx):
    return np.tile(idx.reshape(-1, 16).T, (8, 1)).astype(np.uint16)


def unstriped(offs):
    return offs[:16].T.reshape(-1).astype(np.int64)


E2M1 = np.array([0.0, 0.5, 1.0, 1.5, 2.0, 3.0, 4.0, 6.0, -0.0, -0.5, -1.0, -1.5, -2.0, -3.0, -4.0, -6.0])


def pack_weight(w, fmt):
    k, n = w.shape
    w = f64(np.asarray(w, np.float32).astype(ml_dtypes.bfloat16)).reshape(k // 32, 32, n)
    amax = np.abs(w).max(1)
    if fmt == "e4m3":
        byte = np.frexp(amax)[1] - 1 + 127 - 7
    else:
        mant, ex = np.frexp(amax / 6.0)
        byte = np.where(mant > 0.5, ex, ex - 1) + 127
    byte = np.clip(np.where(amax > 0, byte, 1), 1, 254)
    scaled = (w * np.exp2(127.0 - byte)[:, None, :]).reshape(k, n).astype(np.float32)
    by_word = np.ascontiguousarray(scaled.reshape(k // 512, 128, 4, n).transpose(0, 1, 3, 2))
    if fmt == "e4m3":
        words = by_word.astype(ml_dtypes.float8_e4m3fn).view(np.uint8)
    else:
        c = by_word.astype(ml_dtypes.float4_e2m1fn).view(np.uint8) & 0xF
        words = (c[..., 0::2] | (c[..., 1::2] << 4)).reshape(k // 512, 128, 2 * n)
    return np.ascontiguousarray(words), np.ascontiguousarray(byte.astype(np.uint8).reshape(k // 512, 16, n))


def unpack_weight(words, scales, fmt):
    g, _, n = scales.shape
    words = np.ascontiguousarray(words).reshape(g, 128, n, -1)
    if fmt == "e4m3":
        vals = words.view(ml_dtypes.float8_e4m3fn).astype(np.float64)
    else:
        nib = np.empty((g, 128, n, 4), np.uint8)
        nib[..., 0::2] = words & 0xF
        nib[..., 1::2] = words >> 4
        vals = E2M1[nib]
    vals = vals * np.repeat(np.exp2(scales.astype(np.float64) - 127.0), 8, axis=1)[..., None]
    return vals.transpose(0, 1, 3, 2).reshape(g * 512, n)


def gelu(v):
    return 0.5 * v * (1.0 + np.tanh(np.sqrt(2.0 / np.pi) * (v + 0.044715 * v**3)))


K, T, S, H, T2, N, P = 1536, 4096, 1024, 1024, 2048, 384, 1024

def setup_inputs():
    n = np.random.standard_normal
    s = mx_kscale(K)[:, None]
    u = mx_kscale(H)[:, None]
    d = {}
    d["tab_words"], d["tab_scales"] = pack_weight(n((K, T)) * s, "e4m3")
    d["offs"] = striped(np.random.permutation(T)[:S])
    d["offs2"] = striped(np.random.permutation(T2)[:S])
    d["offs3"] = striped(np.random.permutation(T2)[:P])
    d["offs4"] = striped(np.random.permutation(T2)[:P])
    d["w1"] = (n((K, H)) / K**0.5 / s * u.T).astype(np.float32)
    d["w3_words"], d["w3_scales"] = pack_weight(0.4 * n((K, N)) / K**0.5 / s, "e4m3")
    d["w4_words"], d["w4_scales"] = pack_weight(n((H, N)) / H**0.5 / u, "e2m1")
    d["level"] = (n((H, S)) * u).astype(np.float32)
    d["gain"] = np.exp(0.4 * n(H)).astype(np.float32)
    d["phase"] = np.random.uniform(-1.0, 1.0, N).astype(np.float32)
    d["wgs"] = np.exp(0.3 * n((128, S))).astype(np.float32)
    d["wgo"] = np.exp(0.3 * n((128, P))).astype(np.float32)
    d["page0"] = (n((H, T2)) * u).astype(np.float32)
    d["page1"] = n((N, T2)).astype(np.float32)
    return d

def reference(tab_words, tab_scales, offs, offs2, offs3, offs4, w1, w3_words, w3_scales, w4_words, w4_scales, level, gain, phase, wgs, wgo, page0, page1):
    v = unpack_weight(tab_words, tab_scales, "e4m3")[:, unstriped(offs)]
    h = np.maximum(mxq(f64(w1), 0, "e4m3").T @ v, f64(level))
    page = f64(page0).copy()
    page[:, unstriped(offs2)] = np.tile(f64(wgs), (H // 128, 1)) * h
    x = mxq(page[:, unstriped(offs3)] * f64(gain)[:, None], 0, "e4m3")
    w4 = unpack_weight(w4_words, w4_scales, "e2m1")
    zones = w4.T @ x
    w3 = unpack_weight(w3_words, w3_scales, "e4m3")
    skip = w3.T @ v
    y = zones * np.cos(skip + f64(phase)[:, None])
    out = f64(page1).copy()
    out[:, unstriped(offs4)] = np.tile(f64(wgo), (N // 128, 1)) * y
    return out

@@ -1,0 +1,355 @@
+import math
+from contextlib import ExitStack
+
+import concourse.mybir as mybir
+from concourse.masks import make_identity
+
+K, T, S, H, T2, N = 1536, 4096, 1024, 1024, 2048, 384
+FLOPS = 2 * K * H * S + 2 * K * N * S + 2 * H * N * S
+
+F32 = mybir.dt.float32
+BF16 = mybir.dt.bfloat16
+I32 = mybir.dt.int32
+U32 = mybir.dt.uint32
+U16 = mybir.dt.uint16
+U8 = mybir.dt.uint8
+FP8X4 = mybir.dt.float8_e4m3fn_x4
+FP4X4 = mybir.dt.float4_e2m1fn_x4
+ALU = mybir.AluOpType
+ACT = mybir.ActivationFunctionType
+
+P = 128
+KA = K // 512
+RB = H // 512
+RC = H // P
+NC = N // P
+HALF = 512
+W1_GROUPS = [(0, 1), (1, 2), (2, 4), (4, 6), (6, 8)]
+
+
+def tile_list_wave_pool_paddle_features_kernel(
+    tc, tab_words, tab_scales, offs, offs2, offs3, offs4, w1, w3_words, w3_scales,
+    w4_words, w4_scales, level, gain, phase, wgs, wgo, page0, page1, out,
+):
+    nc = tc.nc
+
+    def cols(h):
+        return slice(h * HALF, (h + 1) * HALF)
+
+    def entries(lst, h):
+        return lst[:, h * HALF // 16 : (h + 1) * HALF // 16]
+
+    with ExitStack() as ctx:
+        keep = ctx.enter_context(tc.tile_pool(name="keep", bufs=1))
+        ring = ctx.enter_context(tc.tile_pool(name="ring", bufs=2))
+        psum = ctx.enter_context(tc.psum_pool(name="psum", bufs=1))
+
+        list1 = keep.tile([P, S // 16], U16, name="list1")
+        list2 = keep.tile([P, S // 16], U16, name="list2")
+        list3 = keep.tile([P, S // 16], U16, name="list3")
+        list4 = keep.tile([P, S // 16], U16, name="list4")
+        v_words = [keep.tile([P, S], U32, name="v_words%d" % a, align_bytes=64) for a in range(KA)]
+        v_scales = keep.tile([P, S], U8, name="v_scales", align_bytes=64)
+
+        w1_raw = {}
+
+        def load_w1(c0):
+            c1 = dict(W1_GROUPS)[c0]
+            for a in range(KA):
+                t = ring.tile([P, 4, (c1 - c0) * P], F32, name="w1_raw", bufs=6)
+                nc.sync.dma_start(
+                    t[:], w1[512 * a : 512 * (a + 1), c0 * P : c1 * P].rearrange("(p i) c -> p i c", i=4)
+                )
+                for c in range(c0, c1):
+                    w1_raw[c, a] = t[:, :, (c - c0) * P : (c - c0 + 1) * P]
+
+        with tc.tile_pool(name="table", bufs=1) as table:
+            t_scales = table.tile([P, T], U8, name="t_scales")
+            t_words = [table.tile([P, T], I32, name="t_words%d" % a) for a in range(KA)]
+
+            def load_table(a):
+                nc.sync.dma_start(t_words[a][:], tab_words[a].rearrange("p t i -> p (t i)").bitcast(I32))
+
+            nc.vector.memset(t_scales[:].bitcast(I32), 0)
+            nc.sync.dma_start(list1[:], offs)
+            nc.sync.dma_start(list2[:], offs2)
+            nc.sync.dma_start(list3[:], offs3)
+            nc.sync.dma_start(list4[:], offs4)
+            load_table(0)
+            load_w1(0)
+            for q in range(4):
+                nc.scalar.dma_start(
+                    t_scales[32 * q : 32 * q + 4 * KA, :].bitcast(I32),
+                    tab_scales[:, 4 * q : 4 * q + 4, :].bitcast(I32),
+                )
+            load_table(1)
+            load_table(2)
+            nc.vector.tensor_copy(v_words[0][:], t_words[0][:].bitcast(U32).indirect(list1[:]))
+            nc.vector.tensor_copy(v_scales[:], t_scales[:].indirect(list1[:]))
+            nc.vector.tensor_copy(v_words[1][:], t_words[1][:].bitcast(U32).indirect(list1[:]))
+            for h in range(2):
+                nc.vector.tensor_copy(v_words[2][:, cols(h)], t_words[2][:].bitcast(U32).indirect(entries(list1, h)))
+
+        late = ctx.enter_context(tc.tile_pool(name="late", bufs=1))
+
+        ident = keep.tile([P, P], F32, name="ident")
+        make_identity(nc, ident[:])
+        ident_b = keep.tile([P, P], BF16, name="ident_b")
+        make_identity(nc, ident_b[:])
+        rows = keep.tile([P, P], F32, name="rows")
+        nc.gpsimd.memset(rows[:], 0.0)
+        w_scales = keep.tile([P, KA + RB, N], U8, name="w_scales", align_bytes=64)
+        nc.gpsimd.memset(w_scales[:].rearrange("p a c -> p (a c)").bitcast(I32), 0)
+
+        wgs_sb = keep.tile([P, S], F32, name="wgs_sb")
+        wgo_sb = keep.tile([P, S], F32, name="wgo_sb")
+        w3_sb = keep.tile([P, KA, N], I32, name="w3_sb", align_bytes=64)
+        w4_sb = keep.tile([P, RB, 2 * N], U8, name="w4_sb", align_bytes=64)
+        chan = keep.tile([P, RC + NC], F32, name="chan")
+        xq = [keep.tile([P, S], U32, name="xq%d" % b, align_bytes=64) for b in range(RB)]
+        stage = keep.tile([P, S], F32, name="stage", align_bytes=64)
+        acc = [psum.tile([P, HALF], F32, name="acc%d" % h) for h in range(2)]
+        skip = psum.tile([P, HALF], F32, name="skip")
+        angle = psum.tile([P, HALF], F32, name="angle")
+        xs = [keep.tile([P, S], U8, name="xs%d" % b, align_bytes=64) for b in range(RB)]
+
+        w1_q, w1_s, lev, page, hh, xT, q_cos, paddle, ys = {}, {}, {}, {}, {}, {}, {}, {}, {}
+
+        def load_level(c):
+            lev[c] = ring.tile([P, S], F32, name="lev", bufs=3)
+            nc.sync.dma_start(lev[c][:], level[c * P : (c + 1) * P, :])
+
+        def load_page(c):
+            page[c] = ring.tile([P, T2], F32, name="page", bufs=4)
+            nc.sync.dma_start(page[c][:], page0[c * P : (c + 1) * P, :])
+
+        def quantise_w1(c):
+            flat = stage[:].bitcast(BF16)
+            wb = flat[:, 0 : KA * 4 * P].rearrange("p (a c i) -> p a c i", a=KA, i=4)
+            for a in range(KA):
+                src = w1_raw[c, a].rearrange("p i c -> p c i")
+                if c == 0:
+                    nc.vector.tensor_copy(wb[:, a], src)
+                else:
+                    nc.scalar.copy(wb[:, a], src)
+            w1_q[c] = ring.tile([P, KA * P], U32, name="w1_q", align_bytes=64)
+            w1_s[c] = ring.tile([P, KA * P], U8, name="w1_s", align_bytes=64)
+            for a0, a1 in ((0, 2), (2, 3)):
+                nc.vector.quantize_mx(
+                    out=w1_q[c][:, a0 * P : a1 * P].bitcast(FP8X4),
+                    scales=w1_s[c][:, a0 * P : a1 * P],
+                    in_=flat[:, a0 * 4 * P : a1 * 4 * P],
+                )
+
+        def product_with_table(bank, words, scales, h):
+            for a in range(KA):
+                nc.tensor.matmul_mx(
+                    out=bank[:],
+                    lhsT=words(a).bitcast(FP8X4),
+                    lhsT_scale=scales(a),
+                    rhs=v_words[a][:, cols(h)].bitcast(FP8X4),
+                    rhs_scale=v_scales[4 * a :, cols(h)],
+                    start=(a == 0),
+                    stop=(a == KA - 1),
+                )
+
+        def first_product(c):
+            for h in range(2):
+                product_with_table(
+                    acc[h],
+                    lambda a: w1_q[c][:, a * P : (a + 1) * P],
+                    lambda a: w1_s[c][:, a * P : (a + 1) * P],
+                    h,
+                )
+
+        def maximum(c, halves=(0, 1)):
+            if c not in hh:
+                hh[c] = ring.tile([P, S], F32, name="hh", align_bytes=64)
+            for h in halves:
+                nc.vector.tensor_tensor(hh[c][:, cols(h)], acc[h][:], lev[c][:, cols(h)], ALU.max)
+
+        def scatter_page(c, h=None):
+            if h is not None:
+                nc.vector.tensor_tensor(
+                    page[c][:].indirect(entries(list2, h)), hh[c][:, cols(h)], wgs_sb[:, cols(h)], ALU.mult
+                )
+            else:
+                nc.vector.tensor_tensor(page[c][:].indirect(list2[:]), hh[c][:], wgs_sb[:], ALU.mult)
+
+        def recall(c, halves, g, xb=None):
+            b, slot = divmod(c, 4)
+            n = HALF * len(halves)
+            j0 = HALF * halves[0]
+            nc.vector.tensor_copy(g, page[c][:].indirect(list3[:, j0 // 16 : (j0 + n) // 16]))
+            if xb is None:
+                xb = ring.tile([P, n], BF16, name="xb")[:]
+            nc.scalar.activation(xb, g, ACT.Copy, scale=chan[:, c : c + 1])
+            for i, h in enumerate(halves):
+                if (b, h) not in xT:
+                    xT[b, h] = ring.tile([P, 4, 512], BF16, name="xT", bufs=4)
+                bank = psum.tile([P, 4, P], BF16, name="t1", bufs=2)
+                for jb in range(4):
+                    j = i * HALF + jb * P
+                    nc.tensor.transpose(bank[:, jb, :], xb[:, j : j + P], ident_b[:])
+                nc.scalar.copy(xT[b, h][:, :, slot * P : (slot + 1) * P], bank[:])
+
+        def quantise_x(b, h, woven):
+            words = xT[b, h][:].bitcast(F32)
+            xi_words = woven[:].rearrange("p (jb j u) -> p jb j u", jb=4, u=2)
+            for pair in range(2):
+                bank = psum.tile([P, 2, 2, P], F32, name="t2", bufs=2)
+                for jj in range(2):
+                    for u in range(2):
+                        nc.tensor.transpose(bank[:, jj, u, :], words[:, 2 * pair + jj, u::2], ident[:])
+                nc.scalar.copy(
+                    xi_words[:, 2 * pair : 2 * pair + 2], bank[:].rearrange("p jj u j -> p jj j u")
+                )
+            nc.vector.quantize_mx(
+                out=xq[b][:, cols(h)].bitcast(FP8X4), scales=xs[b][:, cols(h)], in_=woven[:].bitcast(BF16)
+            )
+
+        def cosine(k, back):
+            n, h = divmod(k, 2)
+            product_with_table(
+                skip,
+                lambda a: w3_sb[:, a, n * P : (n + 1) * P],
+                lambda a: w_scales[:, a, n * P : (n + 1) * P],
+                h,
+            )
+            ang = late.tile([P, HALF], F32, name="ang")
+            nc.scalar.activation(ang[:], skip[:], ACT.Abs, bias=chan[:, RC + n : RC + n + 1])
+            turns = late.tile([P, HALF], U32, name="turns")
+            nc.scalar.activation(turns[:], ang[:], ACT.Copy, scale=1.0 / (2.0 * math.pi), bias=0.75)
+            nc.scalar.activation(back, turns[:], ACT.Copy, scale=-2.0 * math.pi, bias=math.pi)
+            for jb in range(4):
+                blk = slice(jb * P, (jb + 1) * P)
+                nc.tensor.matmul(angle[:, blk], lhsT=back[:, blk], rhs=ident[:], is_transpose=True, start=True, stop=False)
+                nc.tensor.matmul(angle[:, blk], lhsT=ang[:, blk], rhs=ident[:], is_transpose=True, start=False, stop=True)
+            half_cos = late.tile([P, HALF], F32, name="half_cos")
+            nc.scalar.activation(half_cos[:], angle[:], ACT.Sin, scale=0.5)
+            for jb in range(4):
+                blk = slice(jb * P, (jb + 1) * P)
+                nc.tensor.transpose(angle[:, blk], half_cos[:, blk], ident[:])
+            if n not in q_cos:
+                q_cos[n] = late.tile([P, S], F32, name="q_cos%d" % n)
+            nc.scalar.activation(q_cos[n][:, cols(h)], angle[:], ACT.Square, scale=math.sqrt(2.0))
+
+        def second_product(n, h):
+            zones = [acc[0], acc[1], skip, angle][(n + NC * h) % 4]
+            for b in reversed(range(RB)):
+                nc.tensor.matmul_mx(
+                    out=zones[:],
+                    lhsT=w4_sb[:, b, 2 * n * P : 2 * (n + 1) * P].bitcast(FP4X4),
+                    lhsT_scale=w_scales[:, KA + b, n * P : (n + 1) * P],
+                    rhs=xq[b][:, cols(h)].bitcast(FP8X4),
+                    rhs_scale=xs[b][:, cols(h)],
+                    start=(b == RB - 1),
+                    stop=(b == 0),
+                )
+            ys[n, h] = ring.tile([P, HALF], F32, name="y", bufs=3)
+            nc.vector.scalar_tensor_tensor(ys[n, h][:], q_cos[n][:, cols(h)], 1.0, zones[:], ALU.subtract, ALU.mult)
+
+        def scatter_paddle(n, h):
+            nc.vector.tensor_tensor(paddle[n][:].indirect(entries(list4, h)), ys[n, h][:], wgo_sb[:, cols(h)], ALU.mult)
+            if h == 1:
+                nc.sync.dma_start(out[n * P : (n + 1) * P, :], paddle[n][:])
+
+        def load_small(bank):
+            nc.sync.dma_start(rows[0:RC, :], gain.rearrange("(c p) -> c p", p=P))
+            nc.sync.dma_start(rows[RC : RC + NC, :], phase.rearrange("(c p) -> c p", p=P))
+            nc.tensor.transpose(bank[:, 0:P], rows[:], ident[:])
+            nc.scalar.copy(chan[:], bank[:, 0 : RC + NC])
+
+        def load_scales(first, count, src):
+            for q in range(4):
+                nc.sync.dma_start(
+                    w_scales[32 * q : 32 * q + 4, first : first + count, :].bitcast(I32),
+                    src[:, 4 * q : 4 * q + 4, :].rearrange("a r c -> r a c").bitcast(I32),
+                )
+
+        def load_w3():
+            nc.sync.dma_start(w3_sb[:], w3_words.rearrange("a p c i -> p a (c i)").bitcast(I32))
+            load_scales(0, KA, w3_scales)
+
+        def load_w4():
+            nc.sync.dma_start(w4_sb[:].bitcast(I32), w4_words.rearrange("a p c -> p a c").bitcast(I32))
+            load_scales(KA, RB, w4_scales)
+
+        def load_paddle(n):
+            paddle[n] = late.tile([P, T2], F32, name="paddle%d" % n)
+            nc.sync.dma_start(paddle[n][:], page1[n * P : (n + 1) * P, :])
+
+        lev[0] = ring.tile([P, S], F32, name="lev", bufs=3)
+        nc.sync.dma_start(lev[0][:, cols(0)], level[0:P, cols(0)])
+        nc.sync.dma_start(wgs_sb[:, cols(0)], wgs[:, cols(0)])
+        load_page(0)
+        load_w1(1)
+        nc.sync.dma_start(lev[0][:, cols(1)], level[0:P, cols(1)])
+        load_level(1)
+        nc.sync.dma_start(wgs_sb[:, cols(1)], wgs[:, cols(1)])
+        quantise_w1(0)
+        first_product(0)
+        maximum(0, (0,))
+        scatter_page(0, 0)
+        maximum(0, (1,))
+        load_small(acc[1])
+        quantise_w1(1)
+        first_product(1)
+        scatter_page(0, 1)
+        load_w3()
+        load_page(1)
+        load_w1(2)
+        maximum(1)
+        scatter_page(1)
+        cosine(0, late.tile([P, HALF], F32, name="back")[:])
+        cosine(1, stage[:, cols(0)])
+
+        COS_AT = {2: 2, 3: 3, 4: 4, 6: 5}
+        for c in range(2, RC):
+            load_level(c)
+            load_page(c)
+            if c + 2 in dict(W1_GROUPS):
+                load_w1(c + 2)
+            if c == 4:
+                nc.sync.dma_start(wgo_sb[:], wgo)
+                load_w4()
+            if c >= 5:
+                load_paddle(c - 5)
+            quantise_w1(c)
+            first_product(c)
+            if c - 2 < 4:
+                recall(c - 2, (0, 1), stage[:])
+            else:
+                recall(c - 2, (0,), stage[:, cols(0)])
+            maximum(c)
+            scatter_page(c)
+            if c in COS_AT:
+                cosine(COS_AT[c], stage[:, cols(0)])
+            if c == 5:
+                for h in range(2):
+                    quantise_x(0, h, ring.tile([P, S], F32, name="woven", align_bytes=64))
+
+        last = RC - 1
+        recall(last - 1, (0,), stage[:, cols(0)])
+        recall(last, (0,), stage[:, cols(0)])
+        woven = ring.tile([P, S], F32, name="woven", align_bytes=64)
+        quantise_x(1, 0, woven)
+        spent = xT[1, 0]
+        recall(last, (1,), stage[:, cols(1)], spent[:, 0, :])
+        recall(last - 1, (1,), hh[last][:, cols(0)], spent[:, 1, :])
+        recall(last - 2, (1,), hh[last][:, cols(1)], spent[:, 2, :])
+        recall(last - 3, (1,), woven[:, cols(0)], spent[:, 3, :])
+        second_product(0, 0)
+        second_product(1, 0)
+        scatter_paddle(0, 0)
+        woven = ring.tile([P, S], F32, name="woven", align_bytes=64)
+        quantise_x(1, 1, woven)
+        second_product(2, 0)
+        scatter_paddle(1, 0)
+        second_product(0, 1)
+        scatter_paddle(2, 0)
+        second_product(1, 1)
+        scatter_paddle(0, 1)
+        second_product(2, 1)
+        scatter_paddle(1, 1)
+        scatter_paddle(2, 1)

@@ -24,7 +24,6 @@ RB = H // 512
 RC = H // P
 NC = N // P
 HALF = 512
-W1_GROUPS = [(0, 1), (1, 2), (2, 4), (4, 6), (6, 8)]
 
 
 def tile_list_wave_pool_paddle_features_kernel(
@@ -53,15 +52,13 @@ def tile_list_wave_pool_paddle_features_kernel(
 
         w1_raw = {}
 
-        def load_w1(c0):
-            c1 = dict(W1_GROUPS)[c0]
+        def load_w1(c):
+            w1_raw[c] = ring.tile([P, 2 * S], F32, name="w1_raw", bufs=3)
             for a in range(KA):
-                t = ring.tile([P, 4, (c1 - c0) * P], F32, name="w1_raw", bufs=6)
                 nc.sync.dma_start(
-                    t[:], w1[512 * a : 512 * (a + 1), c0 * P : c1 * P].rearrange("(p i) c -> p i c", i=4)
+                    w1_raw[c][:, a * 4 * P : (a + 1) * 4 * P].rearrange("p (i c) -> p i c", i=4),
+                    w1[512 * a : 512 * (a + 1), c * P : (c + 1) * P].rearrange("(p i) c -> p i c", i=4),
                 )
-                for c in range(c0, c1):
-                    w1_raw[c, a] = t[:, :, (c - c0) * P : (c - c0 + 1) * P]
 
         with tc.tile_pool(name="table", bufs=1) as table:
             t_scales = table.tile([P, T], U8, name="t_scales")
@@ -72,17 +69,14 @@ def tile_list_wave_pool_paddle_features_kernel(
 
             nc.vector.memset(t_scales[:].bitcast(I32), 0)
             nc.sync.dma_start(list1[:], offs)
-            nc.sync.dma_start(list2[:], offs2)
-            nc.sync.dma_start(list3[:], offs3)
-            nc.sync.dma_start(list4[:], offs4)
             load_table(0)
-            load_w1(0)
             for q in range(4):
-                nc.scalar.dma_start(
+                nc.sync.dma_start(
                     t_scales[32 * q : 32 * q + 4 * KA, :].bitcast(I32),
                     tab_scales[:, 4 * q : 4 * q + 4, :].bitcast(I32),
                 )
             load_table(1)
+            load_w1(0)
             load_table(2)
             nc.vector.tensor_copy(v_words[0][:], t_words[0][:].bitcast(U32).indirect(list1[:]))
             nc.vector.tensor_copy(v_scales[:], t_scales[:].indirect(list1[:]))
@@ -98,22 +92,24 @@ def tile_list_wave_pool_paddle_features_kernel(
         make_identity(nc, ident_b[:])
         rows = keep.tile([P, P], F32, name="rows")
         nc.gpsimd.memset(rows[:], 0.0)
-        w_scales = keep.tile([P, KA + RB, N], U8, name="w_scales", align_bytes=64)
-        nc.gpsimd.memset(w_scales[:].rearrange("p a c -> p (a c)").bitcast(I32), 0)
+        w3_sc = keep.tile([P, KA, N], U8, name="w3_sc", align_bytes=64)
+        w4_sc = keep.tile([P, RB, N], U8, name="w4_sc", align_bytes=64)
+        for plane in (w3_sc, w4_sc):
+            nc.gpsimd.memset(plane[:].rearrange("p a c -> p (a c)").bitcast(I32), 0)
 
-        wgs_sb = keep.tile([P, S], F32, name="wgs_sb")
+        wgs_sb = keep.tile([P, S], F32, name="wgs_sb", align_bytes=64)
         wgo_sb = keep.tile([P, S], F32, name="wgo_sb")
         w3_sb = keep.tile([P, KA, N], I32, name="w3_sb", align_bytes=64)
         w4_sb = keep.tile([P, RB, 2 * N], U8, name="w4_sb", align_bytes=64)
         chan = keep.tile([P, RC + NC], F32, name="chan")
         xq = [keep.tile([P, S], U32, name="xq%d" % b, align_bytes=64) for b in range(RB)]
-        stage = keep.tile([P, S], F32, name="stage", align_bytes=64)
+        stage = keep.tile([P, KA * 2 * P], F32, name="stage", align_bytes=64)
         acc = [psum.tile([P, HALF], F32, name="acc%d" % h) for h in range(2)]
         skip = psum.tile([P, HALF], F32, name="skip")
         angle = psum.tile([P, HALF], F32, name="angle")
         xs = [keep.tile([P, S], U8, name="xs%d" % b, align_bytes=64) for b in range(RB)]
 
-        w1_q, w1_s, lev, page, hh, xT, q_cos, paddle, ys = {}, {}, {}, {}, {}, {}, {}, {}, {}
+        w1_q, w1_s, lev, page, hh, xT, q_cos, paddle, ys, xbs = {}, {}, {}, {}, {}, {}, {}, {}, {}, {}
 
         def load_level(c):
             lev[c] = ring.tile([P, S], F32, name="lev", bufs=3)
@@ -123,11 +119,11 @@ def tile_list_wave_pool_paddle_features_kernel(
             page[c] = ring.tile([P, T2], F32, name="page", bufs=4)
             nc.sync.dma_start(page[c][:], page0[c * P : (c + 1) * P, :])
 
-        def quantise_w1(c):
-            flat = stage[:].bitcast(BF16)
+        def quantise_w1(c, staging):
+            flat = staging.bitcast(BF16)
             wb = flat[:, 0 : KA * 4 * P].rearrange("p (a c i) -> p a c i", a=KA, i=4)
             for a in range(KA):
-                src = w1_raw[c, a].rearrange("p i c -> p c i")
+                src = w1_raw[c][:, a * 4 * P : (a + 1) * 4 * P].rearrange("p (i c) -> p c i", i=4)
                 if c == 0:
                     nc.vector.tensor_copy(wb[:, a], src)
                 else:
@@ -163,8 +159,10 @@ def tile_list_wave_pool_paddle_features_kernel(
                 )
 
         def maximum(c, halves=(0, 1)):
-            if c not in hh:
-                hh[c] = ring.tile([P, S], F32, name="hh", align_bytes=64)
+            if 2 <= c < RC - 1:
+                hh[c] = w1_raw[c + 1][:, 0:S]
+            elif c not in hh:
+                hh[c] = ring.tile([P, S], F32, name="woven", bufs=3, align_bytes=64)[:]
             for h in halves:
                 nc.vector.tensor_tensor(hh[c][:, cols(h)], acc[h][:], lev[c][:, cols(h)], ALU.max)
 
@@ -174,16 +172,20 @@ def tile_list_wave_pool_paddle_features_kernel(
                     page[c][:].indirect(entries(list2, h)), hh[c][:, cols(h)], wgs_sb[:, cols(h)], ALU.mult
                 )
             else:
-                nc.vector.tensor_tensor(page[c][:].indirect(list2[:]), hh[c][:], wgs_sb[:], ALU.mult)
+                nc.vector.tensor_tensor(page[c][:].indirect(list2[:]), hh[c], wgs_sb[:], ALU.mult)
 
         def recall(c, halves, g, xb=None):
-            b, slot = divmod(c, 4)
             n = HALF * len(halves)
             j0 = HALF * halves[0]
             nc.vector.tensor_copy(g, page[c][:].indirect(list3[:, j0 // 16 : (j0 + n) // 16]))
             if xb is None:
                 xb = ring.tile([P, n], BF16, name="xb")[:]
             nc.scalar.activation(xb, g, ACT.Copy, scale=chan[:, c : c + 1])
+            xbs[c] = (halves, xb)
+
+        def turn(c):
+            b, slot = divmod(c, 4)
+            halves, xb = xbs[c]
             for i, h in enumerate(halves):
                 if (b, h) not in xT:
                     xT[b, h] = ring.tile([P, 4, 512], BF16, name="xT", bufs=4)
@@ -196,8 +198,8 @@ def tile_list_wave_pool_paddle_features_kernel(
         def quantise_x(b, h, woven):
             words = xT[b, h][:].bitcast(F32)
             xi_words = woven[:].rearrange("p (jb j u) -> p jb j u", jb=4, u=2)
-            for pair in range(2):
-                bank = psum.tile([P, 2, 2, P], F32, name="t2", bufs=2)
+            banks = [psum.tile([P, 2, 2, P], F32, name="t2", bufs=2) for pair in range(2)]
+            for pair, bank in enumerate(banks):
                 for jj in range(2):
                     for u in range(2):
                         nc.tensor.transpose(bank[:, jj, u, :], words[:, 2 * pair + jj, u::2], ident[:])
@@ -207,50 +209,58 @@ def tile_list_wave_pool_paddle_features_kernel(
             nc.vector.quantize_mx(
                 out=xq[b][:, cols(h)].bitcast(FP8X4), scales=xs[b][:, cols(h)], in_=woven[:].bitcast(BF16)
             )
+            return banks[0][:].rearrange("p jj u j -> p (jj u j)")
 
-        def cosine(k, back):
-            n, h = divmod(k, 2)
+        def cosine(k, back, ang=None):
+            h, n = divmod(k, NC)
             product_with_table(
                 skip,
                 lambda a: w3_sb[:, a, n * P : (n + 1) * P],
-                lambda a: w_scales[:, a, n * P : (n + 1) * P],
+                lambda a: w3_sc[:, a, n * P : (n + 1) * P],
                 h,
             )
-            ang = late.tile([P, HALF], F32, name="ang")
-            nc.scalar.activation(ang[:], skip[:], ACT.Abs, bias=chan[:, RC + n : RC + n + 1])
+            if ang is None:
+                ang = late.tile([P, HALF], F32, name="ang")[:]
+            nc.scalar.activation(ang, skip[:], ACT.Abs, bias=chan[:, RC + n : RC + n + 1])
             turns = late.tile([P, HALF], U32, name="turns")
-            nc.scalar.activation(turns[:], ang[:], ACT.Copy, scale=1.0 / (2.0 * math.pi), bias=0.75)
-            nc.scalar.activation(back, turns[:], ACT.Copy, scale=-2.0 * math.pi, bias=math.pi)
+            nc.scalar.activation(turns[:], ang, ACT.Copy, scale=1.0 / (2.0 * math.pi))
+            nc.scalar.activation(back, turns[:], ACT.Copy, scale=-2.0 * math.pi)
             for jb in range(4):
                 blk = slice(jb * P, (jb + 1) * P)
                 nc.tensor.matmul(angle[:, blk], lhsT=back[:, blk], rhs=ident[:], is_transpose=True, start=True, stop=False)
                 nc.tensor.matmul(angle[:, blk], lhsT=ang[:, blk], rhs=ident[:], is_transpose=True, start=False, stop=True)
-            half_cos = late.tile([P, HALF], F32, name="half_cos")
-            nc.scalar.activation(half_cos[:], angle[:], ACT.Sin, scale=0.5)
+            rest = late.tile([P, HALF], F32, name="rest")
+            nc.scalar.activation(rest[:], angle[:], ACT.Abs)
             for jb in range(4):
                 blk = slice(jb * P, (jb + 1) * P)
-                nc.tensor.transpose(angle[:, blk], half_cos[:, blk], ident[:])
+                nc.tensor.transpose(angle[:, blk], rest[:, blk], ident[:])
+            cos_k = late.tile([P, HALF], F32, name="cos_k", bufs=2)
+            nc.scalar.activation(cos_k[:], angle[:], ACT.Sin, scale=-1.0, bias=0.5 * math.pi)
             if n not in q_cos:
                 q_cos[n] = late.tile([P, S], F32, name="q_cos%d" % n)
-            nc.scalar.activation(q_cos[n][:, cols(h)], angle[:], ACT.Square, scale=math.sqrt(2.0))
+            nc.gpsimd.tensor_tensor(q_cos[n][:, cols(h)], cos_k[:], wgo_sb[:, cols(h)], ALU.mult)
 
-        def second_product(n, h):
-            zones = [acc[0], acc[1], skip, angle][(n + NC * h) % 4]
+        def second_product(n, h, zones):
             for b in reversed(range(RB)):
                 nc.tensor.matmul_mx(
-                    out=zones[:],
+                    out=zones,
                     lhsT=w4_sb[:, b, 2 * n * P : 2 * (n + 1) * P].bitcast(FP4X4),
-                    lhsT_scale=w_scales[:, KA + b, n * P : (n + 1) * P],
+                    lhsT_scale=w4_sc[:, b, n * P : (n + 1) * P],
                     rhs=xq[b][:, cols(h)].bitcast(FP8X4),
                     rhs_scale=xs[b][:, cols(h)],
                     start=(b == RB - 1),
                     stop=(b == 0),
                 )
-            ys[n, h] = ring.tile([P, HALF], F32, name="y", bufs=3)
-            nc.vector.scalar_tensor_tensor(ys[n, h][:], q_cos[n][:, cols(h)], 1.0, zones[:], ALU.subtract, ALU.mult)
+            ys[n, h] = ring.tile([P, HALF], F32, name="y", bufs=3)[:]
+            if n + h == 0:
+                nc.vector.tensor_copy(ys[n, h], zones)
+            else:
+                nc.scalar.copy(ys[n, h], zones)
 
         def scatter_paddle(n, h):
-            nc.vector.tensor_tensor(paddle[n][:].indirect(entries(list4, h)), ys[n, h][:], wgo_sb[:, cols(h)], ALU.mult)
+            nc.vector.tensor_tensor(
+                paddle[n][:].indirect(entries(list4, h)), ys[n, h], q_cos[n][:, cols(h)], ALU.mult
+            )
             if h == 1:
                 nc.sync.dma_start(out[n * P : (n + 1) * P, :], paddle[n][:])
 
@@ -260,26 +270,27 @@ def tile_list_wave_pool_paddle_features_kernel(
             nc.tensor.transpose(bank[:, 0:P], rows[:], ident[:])
             nc.scalar.copy(chan[:], bank[:, 0 : RC + NC])
 
-        def load_scales(first, count, src):
+        def load_scales(plane, src):
             for q in range(4):
                 nc.sync.dma_start(
-                    w_scales[32 * q : 32 * q + 4, first : first + count, :].bitcast(I32),
+                    plane[32 * q : 32 * q + 4].bitcast(I32),
                     src[:, 4 * q : 4 * q + 4, :].rearrange("a r c -> r a c").bitcast(I32),
                 )
 
         def load_w3():
             nc.sync.dma_start(w3_sb[:], w3_words.rearrange("a p c i -> p a (c i)").bitcast(I32))
-            load_scales(0, KA, w3_scales)
+            load_scales(w3_sc, w3_scales)
 
         def load_w4():
             nc.sync.dma_start(w4_sb[:].bitcast(I32), w4_words.rearrange("a p c -> p a c").bitcast(I32))
-            load_scales(KA, RB, w4_scales)
+            load_scales(w4_sc, w4_scales)
 
         def load_paddle(n):
             paddle[n] = late.tile([P, T2], F32, name="paddle%d" % n)
             nc.sync.dma_start(paddle[n][:], page1[n * P : (n + 1) * P, :])
 
         lev[0] = ring.tile([P, S], F32, name="lev", bufs=3)
+        nc.sync.dma_start(list2[:], offs2)
         nc.sync.dma_start(lev[0][:, cols(0)], level[0:P, cols(0)])
         nc.sync.dma_start(wgs_sb[:, cols(0)], wgs[:, cols(0)])
         load_page(0)
@@ -287,69 +298,85 @@ def tile_list_wave_pool_paddle_features_kernel(
         nc.sync.dma_start(lev[0][:, cols(1)], level[0:P, cols(1)])
         load_level(1)
         nc.sync.dma_start(wgs_sb[:, cols(1)], wgs[:, cols(1)])
-        quantise_w1(0)
+        quantise_w1(0, stage[:])
         first_product(0)
         maximum(0, (0,))
         scatter_page(0, 0)
         maximum(0, (1,))
         load_small(acc[1])
-        quantise_w1(1)
+        quantise_w1(1, stage[:])
         first_product(1)
         scatter_page(0, 1)
         load_w3()
         load_page(1)
         load_w1(2)
+        load_w1(3)
+        nc.sync.dma_start(wgo_sb[:], wgo)
+        nc.sync.dma_start(list3[:], offs3)
         maximum(1)
         scatter_page(1)
-        cosine(0, late.tile([P, HALF], F32, name="back")[:])
-        cosine(1, stage[:, cols(0)])
+        middle = slice(256, 768)
+        extra = ring.tile([P, S], F32, name="woven", bufs=3, align_bytes=64)
+        cosine(0, extra[:, middle])
+        quantise_w1(2, extra[:])
+        first_product(2)
 
-        COS_AT = {2: 2, 3: 3, 4: 4, 6: 5}
         for c in range(2, RC):
             load_level(c)
             load_page(c)
-            if c + 2 in dict(W1_GROUPS):
+            if c + 2 < RC:
                 load_w1(c + 2)
             if c == 4:
-                nc.sync.dma_start(wgo_sb[:], wgo)
+                nc.sync.dma_start(list4[:], offs4)
                 load_w4()
             if c >= 5:
                 load_paddle(c - 5)
-            quantise_w1(c)
-            first_product(c)
-            if c - 2 < 4:
-                recall(c - 2, (0, 1), stage[:])
+            if c + 1 < RC:
+                if c > 2:
+                    cosine(c - 2, stage[:, middle])
+                quantise_w1(c + 1, stage[:])
+                if c > 2:
+                    turn(c - 3)
+                spent = w1_raw[c + 1 if c > 2 else c][:, S:]
+                if c - 2 < 4:
+                    recall(c - 2, (0, 1), spent)
+                else:
+                    recall(c - 2, (0,), spent[:, cols(0)])
             else:
-                recall(c - 2, (0,), stage[:, cols(0)])
+                hh[c] = ring.tile([P, S], F32, name="woven", bufs=3, align_bytes=64)[:]
+                cosine(c - 2, spent[:, middle], hh[c][:, cols(1)])
+                turn(c - 3)
+                for d in range(2):
+                    recall(c - 2 + d, (0,), spent[:, cols(d)])
+                    turn(c - 2 + d)
             maximum(c)
+            if c + 1 < RC:
+                first_product(c + 1)
             scatter_page(c)
-            if c in COS_AT:
-                cosine(COS_AT[c], stage[:, cols(0)])
-            if c == 5:
-                for h in range(2):
-                    quantise_x(0, h, ring.tile([P, S], F32, name="woven", align_bytes=64))
+            if c == 6:
+                quantise_x(0, 0, ring.tile([P, S], F32, name="woven", bufs=3, align_bytes=64))
 
         last = RC - 1
-        recall(last - 1, (0,), stage[:, cols(0)])
-        recall(last, (0,), stage[:, cols(0)])
-        woven = ring.tile([P, S], F32, name="woven", align_bytes=64)
+        free = hh[last - 1]
+        recall(last, (0,), free[:, cols(0)])
+        turn(last)
+        quantise_x(0, 1, wgs_sb)
+        woven = ring.tile([P, S], F32, name="woven", bufs=3, align_bytes=64)
         quantise_x(1, 0, woven)
-        spent = xT[1, 0]
-        recall(last, (1,), stage[:, cols(1)], spent[:, 0, :])
-        recall(last - 1, (1,), hh[last][:, cols(0)], spent[:, 1, :])
-        recall(last - 2, (1,), hh[last][:, cols(1)], spent[:, 2, :])
-        recall(last - 3, (1,), woven[:, cols(0)], spent[:, 3, :])
-        second_product(0, 0)
-        second_product(1, 0)
+        second_product(0, 0, acc[0][:])
+        second_product(1, 0, acc[1][:])
+        halves = woven[:].bitcast(BF16)
+        later = (free[:, cols(1)], hh[last][:, cols(0)], hh[last][:, cols(1)], woven[:, cols(0)])
+        for d in range(4):
+            recall(last - d, (1,), later[d], halves[:, cols(2 + d % 2)] if d else xT[1, 0][:, 0, :])
+            turn(last - d)
         scatter_paddle(0, 0)
-        woven = ring.tile([P, S], F32, name="woven", align_bytes=64)
-        quantise_x(1, 1, woven)
-        second_product(2, 0)
         scatter_paddle(1, 0)
-        second_product(0, 1)
+        bank = quantise_x(1, 1, ring.tile([P, S], F32, name="woven", bufs=3, align_bytes=64))
+        second_product(2, 0, bank)
+        second_product(0, 1, acc[0][:])
         scatter_paddle(2, 0)
-        second_product(1, 1)
-        scatter_paddle(0, 1)
-        second_product(2, 1)
-        scatter_paddle(1, 1)
-        scatter_paddle(2, 1)
+        second_product(1, 1, acc[1][:])
+        second_product(2, 1, skip[:])
+        for n in range(NC):
+            scatter_paddle(n, 1)

import math
from contextlib import ExitStack

import concourse.mybir as mybir
from concourse.masks import make_identity

K, T, S, H, T2, N = 1536, 4096, 1024, 1024, 2048, 384
FLOPS = 2 * K * H * S + 2 * K * N * S + 2 * H * N * S

F32 = mybir.dt.float32
BF16 = mybir.dt.bfloat16
I32 = mybir.dt.int32
U32 = mybir.dt.uint32
U16 = mybir.dt.uint16
U8 = mybir.dt.uint8
FP8X4 = mybir.dt.float8_e4m3fn_x4
FP4X4 = mybir.dt.float4_e2m1fn_x4
ALU = mybir.AluOpType
ACT = mybir.ActivationFunctionType

P = 128
KA = K // 512
RB = H // 512
RC = H // P
NC = N // P
HALF = 512


def tile_list_wave_pool_paddle_features_kernel(
    tc, tab_words, tab_scales, offs, offs2, offs3, offs4, w1, w3_words, w3_scales,
    w4_words, w4_scales, level, gain, phase, wgs, wgo, page0, page1, out,
):
    nc = tc.nc

    def cols(h):
        return slice(h * HALF, (h + 1) * HALF)

    def entries(lst, h):
        return lst[:, h * HALF // 16 : (h + 1) * HALF // 16]

    with ExitStack() as ctx:
        keep = ctx.enter_context(tc.tile_pool(name="keep", bufs=1))
        ring = ctx.enter_context(tc.tile_pool(name="ring", bufs=2))
        psum = ctx.enter_context(tc.psum_pool(name="psum", bufs=1))

        list1 = keep.tile([P, S // 16], U16, name="list1")
        list2 = keep.tile([P, S // 16], U16, name="list2")
        list3 = keep.tile([P, S // 16], U16, name="list3")
        list4 = keep.tile([P, S // 16], U16, name="list4")
        v_words = [keep.tile([P, S], U32, name="v_words%d" % a, align_bytes=64) for a in range(KA)]
        v_scales = keep.tile([P, S], U8, name="v_scales", align_bytes=64)

        w1_raw = {}

        def load_w1(c):
            w1_raw[c] = ring.tile([P, 2 * S], F32, name="w1_raw", bufs=3)
            for a in range(KA):
                nc.sync.dma_start(
                    w1_raw[c][:, a * 4 * P : (a + 1) * 4 * P].rearrange("p (i c) -> p i c", i=4),
                    w1[512 * a : 512 * (a + 1), c * P : (c + 1) * P].rearrange("(p i) c -> p i c", i=4),
                )

        with tc.tile_pool(name="table", bufs=1) as table:
            t_scales = table.tile([P, T], U8, name="t_scales")
            t_words = [table.tile([P, T], I32, name="t_words%d" % a) for a in range(KA)]

            def load_table(a):
                nc.sync.dma_start(t_words[a][:], tab_words[a].rearrange("p t i -> p (t i)").bitcast(I32))

            nc.vector.memset(t_scales[:].bitcast(I32), 0)
            nc.sync.dma_start(list1[:], offs)
            load_table(0)
            for q in range(4):
                nc.sync.dma_start(
                    t_scales[32 * q : 32 * q + 4 * KA, :].bitcast(I32),
                    tab_scales[:, 4 * q : 4 * q + 4, :].bitcast(I32),
                )
            load_table(1)
            load_w1(0)
            load_table(2)
            nc.vector.tensor_copy(v_words[0][:], t_words[0][:].bitcast(U32).indirect(list1[:]))
            nc.vector.tensor_copy(v_scales[:], t_scales[:].indirect(list1[:]))
            nc.vector.tensor_copy(v_words[1][:], t_words[1][:].bitcast(U32).indirect(list1[:]))
            for h in range(2):
                nc.vector.tensor_copy(v_words[2][:, cols(h)], t_words[2][:].bitcast(U32).indirect(entries(list1, h)))

        late = ctx.enter_context(tc.tile_pool(name="late", bufs=1))

        ident = keep.tile([P, P], F32, name="ident")
        make_identity(nc, ident[:])
        ident_b = keep.tile([P, P], BF16, name="ident_b")
        make_identity(nc, ident_b[:])
        rows = keep.tile([P, P], F32, name="rows")
        nc.gpsimd.memset(rows[:], 0.0)
        w3_sc = keep.tile([P, KA, N], U8, name="w3_sc", align_bytes=64)
        w4_sc = keep.tile([P, RB, N], U8, name="w4_sc", align_bytes=64)
        for plane in (w3_sc, w4_sc):
            nc.gpsimd.memset(plane[:].rearrange("p a c -> p (a c)").bitcast(I32), 0)

        wgs_sb = keep.tile([P, S], F32, name="wgs_sb", align_bytes=64)
        wgo_sb = keep.tile([P, S], F32, name="wgo_sb")
        w3_sb = keep.tile([P, KA, N], I32, name="w3_sb", align_bytes=64)
        w4_sb = keep.tile([P, RB, 2 * N], U8, name="w4_sb", align_bytes=64)
        chan = keep.tile([P, RC + NC], F32, name="chan")
        xq = [keep.tile([P, S], U32, name="xq%d" % b, align_bytes=64) for b in range(RB)]
        stage = keep.tile([P, KA * 2 * P], F32, name="stage", align_bytes=64)
        acc = [psum.tile([P, HALF], F32, name="acc%d" % h) for h in range(2)]
        skip = psum.tile([P, HALF], F32, name="skip")
        angle = psum.tile([P, HALF], F32, name="angle")
        xs = [keep.tile([P, S], U8, name="xs%d" % b, align_bytes=64) for b in range(RB)]

        w1_q, w1_s, lev, page, hh, xT, q_cos, paddle, ys, xbs = {}, {}, {}, {}, {}, {}, {}, {}, {}, {}

        def load_level(c):
            lev[c] = ring.tile([P, S], F32, name="lev", bufs=3)
            nc.sync.dma_start(lev[c][:], level[c * P : (c + 1) * P, :])

        def load_page(c):
            page[c] = ring.tile([P, T2], F32, name="page", bufs=4)
            nc.sync.dma_start(page[c][:], page0[c * P : (c + 1) * P, :])

        def quantise_w1(c, staging):
            flat = staging.bitcast(BF16)
            wb = flat[:, 0 : KA * 4 * P].rearrange("p (a c i) -> p a c i", a=KA, i=4)
            for a in range(KA):
                src = w1_raw[c][:, a * 4 * P : (a + 1) * 4 * P].rearrange("p (i c) -> p c i", i=4)
                if c == 0:
                    nc.vector.tensor_copy(wb[:, a], src)
                else:
                    nc.scalar.copy(wb[:, a], src)
            w1_q[c] = ring.tile([P, KA * P], U32, name="w1_q", align_bytes=64)
            w1_s[c] = ring.tile([P, KA * P], U8, name="w1_s", align_bytes=64)
            for a0, a1 in ((0, 2), (2, 3)):
                nc.vector.quantize_mx(
                    out=w1_q[c][:, a0 * P : a1 * P].bitcast(FP8X4),
                    scales=w1_s[c][:, a0 * P : a1 * P],
                    in_=flat[:, a0 * 4 * P : a1 * 4 * P],
                )

        def product_with_table(bank, words, scales, h):
            for a in range(KA):
                nc.tensor.matmul_mx(
                    out=bank[:],
                    lhsT=words(a).bitcast(FP8X4),
                    lhsT_scale=scales(a),
                    rhs=v_words[a][:, cols(h)].bitcast(FP8X4),
                    rhs_scale=v_scales[4 * a :, cols(h)],
                    start=(a == 0),
                    stop=(a == KA - 1),
                )

        def first_product(c):
            for h in range(2):
                product_with_table(
                    acc[h],
                    lambda a: w1_q[c][:, a * P : (a + 1) * P],
                    lambda a: w1_s[c][:, a * P : (a + 1) * P],
                    h,
                )

        def maximum(c, halves=(0, 1)):
            if 2 <= c < RC - 1:
                hh[c] = w1_raw[c + 1][:, 0:S]
            elif c not in hh:
                hh[c] = ring.tile([P, S], F32, name="woven", bufs=3, align_bytes=64)[:]
            for h in halves:
                nc.vector.tensor_tensor(hh[c][:, cols(h)], acc[h][:], lev[c][:, cols(h)], ALU.max)

        def scatter_page(c, h=None):
            if h is not None:
                nc.vector.tensor_tensor(
                    page[c][:].indirect(entries(list2, h)), hh[c][:, cols(h)], wgs_sb[:, cols(h)], ALU.mult
                )
            else:
                nc.vector.tensor_tensor(page[c][:].indirect(list2[:]), hh[c], wgs_sb[:], ALU.mult)

        def recall(c, halves, g, xb=None):
            n = HALF * len(halves)
            j0 = HALF * halves[0]
            nc.vector.tensor_copy(g, page[c][:].indirect(list3[:, j0 // 16 : (j0 + n) // 16]))
            if xb is None:
                xb = ring.tile([P, n], BF16, name="xb")[:]
            nc.scalar.activation(xb, g, ACT.Copy, scale=chan[:, c : c + 1])
            xbs[c] = (halves, xb)

        def turn(c):
            b, slot = divmod(c, 4)
            halves, xb = xbs[c]
            for i, h in enumerate(halves):
                if (b, h) not in xT:
                    xT[b, h] = ring.tile([P, 4, 512], BF16, name="xT", bufs=4)
                bank = psum.tile([P, 4, P], BF16, name="t1", bufs=2)
                for jb in range(4):
                    j = i * HALF + jb * P
                    nc.tensor.transpose(bank[:, jb, :], xb[:, j : j + P], ident_b[:])
                nc.scalar.copy(xT[b, h][:, :, slot * P : (slot + 1) * P], bank[:])

        def quantise_x(b, h, woven):
            words = xT[b, h][:].bitcast(F32)
            xi_words = woven[:].rearrange("p (jb j u) -> p jb j u", jb=4, u=2)
            banks = [psum.tile([P, 2, 2, P], F32, name="t2", bufs=2) for pair in range(2)]
            for pair, bank in enumerate(banks):
                for jj in range(2):
                    for u in range(2):
                        nc.tensor.transpose(bank[:, jj, u, :], words[:, 2 * pair + jj, u::2], ident[:])
                nc.scalar.copy(
                    xi_words[:, 2 * pair : 2 * pair + 2], bank[:].rearrange("p jj u j -> p jj j u")
                )
            nc.vector.quantize_mx(
                out=xq[b][:, cols(h)].bitcast(FP8X4), scales=xs[b][:, cols(h)], in_=woven[:].bitcast(BF16)
            )
            return banks[0][:].rearrange("p jj u j -> p (jj u j)")

        def cosine(k, back, ang=None):
            h, n = divmod(k, NC)
            product_with_table(
                skip,
                lambda a: w3_sb[:, a, n * P : (n + 1) * P],
                lambda a: w3_sc[:, a, n * P : (n + 1) * P],
                h,
            )
            if ang is None:
                ang = late.tile([P, HALF], F32, name="ang")[:]
            nc.scalar.activation(ang, skip[:], ACT.Abs, bias=chan[:, RC + n : RC + n + 1])
            turns = late.tile([P, HALF], U32, name="turns")
            nc.scalar.activation(turns[:], ang, ACT.Copy, scale=1.0 / (2.0 * math.pi))
            nc.scalar.activation(back, turns[:], ACT.Copy, scale=-2.0 * math.pi)
            for jb in range(4):
                blk = slice(jb * P, (jb + 1) * P)
                nc.tensor.matmul(angle[:, blk], lhsT=back[:, blk], rhs=ident[:], is_transpose=True, start=True, stop=False)
                nc.tensor.matmul(angle[:, blk], lhsT=ang[:, blk], rhs=ident[:], is_transpose=True, start=False, stop=True)
            rest = late.tile([P, HALF], F32, name="rest")
            nc.scalar.activation(rest[:], angle[:], ACT.Abs)
            for jb in range(4):
                blk = slice(jb * P, (jb + 1) * P)
                nc.tensor.transpose(angle[:, blk], rest[:, blk], ident[:])
            cos_k = late.tile([P, HALF], F32, name="cos_k", bufs=2)
            nc.scalar.activation(cos_k[:], angle[:], ACT.Sin, scale=-1.0, bias=0.5 * math.pi)
            if n not in q_cos:
                q_cos[n] = late.tile([P, S], F32, name="q_cos%d" % n)
            nc.gpsimd.tensor_tensor(q_cos[n][:, cols(h)], cos_k[:], wgo_sb[:, cols(h)], ALU.mult)

        def second_product(n, h, zones):
            for b in reversed(range(RB)):
                nc.tensor.matmul_mx(
                    out=zones,
                    lhsT=w4_sb[:, b, 2 * n * P : 2 * (n + 1) * P].bitcast(FP4X4),
                    lhsT_scale=w4_sc[:, b, n * P : (n + 1) * P],
                    rhs=xq[b][:, cols(h)].bitcast(FP8X4),
                    rhs_scale=xs[b][:, cols(h)],
                    start=(b == RB - 1),
                    stop=(b == 0),
                )
            ys[n, h] = ring.tile([P, HALF], F32, name="y", bufs=3)[:]
            if n + h == 0:
                nc.vector.tensor_copy(ys[n, h], zones)
            else:
                nc.scalar.copy(ys[n, h], zones)

        def scatter_paddle(n, h):
            nc.vector.tensor_tensor(
                paddle[n][:].indirect(entries(list4, h)), ys[n, h], q_cos[n][:, cols(h)], ALU.mult
            )
            if h == 1:
                nc.sync.dma_start(out[n * P : (n + 1) * P, :], paddle[n][:])

        def load_small(bank):
            nc.sync.dma_start(rows[0:RC, :], gain.rearrange("(c p) -> c p", p=P))
            nc.sync.dma_start(rows[RC : RC + NC, :], phase.rearrange("(c p) -> c p", p=P))
            nc.tensor.transpose(bank[:, 0:P], rows[:], ident[:])
            nc.scalar.copy(chan[:], bank[:, 0 : RC + NC])

        def load_scales(plane, src):
            for q in range(4):
                nc.sync.dma_start(
                    plane[32 * q : 32 * q + 4].bitcast(I32),
                    src[:, 4 * q : 4 * q + 4, :].rearrange("a r c -> r a c").bitcast(I32),
                )

        def load_w3():
            nc.sync.dma_start(w3_sb[:], w3_words.rearrange("a p c i -> p a (c i)").bitcast(I32))
            load_scales(w3_sc, w3_scales)

        def load_w4():
            nc.sync.dma_start(w4_sb[:].bitcast(I32), w4_words.rearrange("a p c -> p a c").bitcast(I32))
            load_scales(w4_sc, w4_scales)

        def load_paddle(n):
            paddle[n] = late.tile([P, T2], F32, name="paddle%d" % n)
            nc.sync.dma_start(paddle[n][:], page1[n * P : (n + 1) * P, :])

        lev[0] = ring.tile([P, S], F32, name="lev", bufs=3)
        nc.sync.dma_start(list2[:], offs2)
        nc.sync.dma_start(lev[0][:, cols(0)], level[0:P, cols(0)])
        nc.sync.dma_start(wgs_sb[:, cols(0)], wgs[:, cols(0)])
        load_page(0)
        load_w1(1)
        nc.sync.dma_start(lev[0][:, cols(1)], level[0:P, cols(1)])
        load_level(1)
        nc.sync.dma_start(wgs_sb[:, cols(1)], wgs[:, cols(1)])
        quantise_w1(0, stage[:])
        first_product(0)
        maximum(0, (0,))
        scatter_page(0, 0)
        maximum(0, (1,))
        load_small(acc[1])
        quantise_w1(1, stage[:])
        first_product(1)
        scatter_page(0, 1)
        load_w3()
        load_page(1)
        load_w1(2)
        load_w1(3)
        nc.sync.dma_start(wgo_sb[:], wgo)
        nc.sync.dma_start(list3[:], offs3)
        maximum(1)
        scatter_page(1)
        middle = slice(256, 768)
        extra = ring.tile([P, S], F32, name="woven", bufs=3, align_bytes=64)
        cosine(0, extra[:, middle])
        quantise_w1(2, extra[:])
        first_product(2)

        for c in range(2, RC):
            load_level(c)
            load_page(c)
            if c + 2 < RC:
                load_w1(c + 2)
            if c == 4:
                nc.sync.dma_start(list4[:], offs4)
                load_w4()
            if c >= 5:
                load_paddle(c - 5)
            if c + 1 < RC:
                if c > 2:
                    cosine(c - 2, stage[:, middle])
                quantise_w1(c + 1, stage[:])
                if c > 2:
                    turn(c - 3)
                spent = w1_raw[c + 1 if c > 2 else c][:, S:]
                if c - 2 < 4:
                    recall(c - 2, (0, 1), spent)
                else:
                    recall(c - 2, (0,), spent[:, cols(0)])
            else:
                hh[c] = ring.tile([P, S], F32, name="woven", bufs=3, align_bytes=64)[:]
                cosine(c - 2, spent[:, middle], hh[c][:, cols(1)])
                turn(c - 3)
                for d in range(2):
                    recall(c - 2 + d, (0,), spent[:, cols(d)])
                    turn(c - 2 + d)
            maximum(c)
            if c + 1 < RC:
                first_product(c + 1)
            scatter_page(c)
            if c == 6:
                quantise_x(0, 0, ring.tile([P, S], F32, name="woven", bufs=3, align_bytes=64))

        last = RC - 1
        free = hh[last - 1]
        recall(last, (0,), free[:, cols(0)])
        turn(last)
        quantise_x(0, 1, wgs_sb)
        woven = ring.tile([P, S], F32, name="woven", bufs=3, align_bytes=64)
        quantise_x(1, 0, woven)
        second_product(0, 0, acc[0][:])
        second_product(1, 0, acc[1][:])
        halves = woven[:].bitcast(BF16)
        later = (free[:, cols(1)], hh[last][:, cols(0)], hh[last][:, cols(1)], woven[:, cols(0)])
        for d in range(4):
            recall(last - d, (1,), later[d], halves[:, cols(2 + d % 2)] if d else xT[1, 0][:, 0, :])
            turn(last - d)
        scatter_paddle(0, 0)
        scatter_paddle(1, 0)
        bank = quantise_x(1, 1, ring.tile([P, S], F32, name="woven", bufs=3, align_bytes=64))
        second_product(2, 0, bank)
        second_product(0, 1, acc[0][:])
        scatter_paddle(2, 0)
        second_product(1, 1, acc[1][:])
        second_product(2, 1, skip[:])
        for n in range(NC):
            scatter_paddle(n, 1)
